import numpy as np, ml_dtypes
CORES = [10,34,74,98]
N = 4
import mx_ref
BF = ml_dtypes.bfloat16
def gentries(a):
    return np.ascontiguousarray(a.reshape(8, 16, -1).transpose(0, 2, 1)).reshape(8, -1)
def gtable(e):
    e = np.asarray(e); return np.ascontiguousarray(e.reshape(8, -1, 16).transpose(0, 2, 1)).reshape(128, -1).astype(np.int32)
def gcols(t, e):
    v = np.concatenate([t.reshape(8, 16, -1, 4), np.zeros((8, 16, 1, 4), BF)], axis=2)
    return np.ascontiguousarray(np.stack([v[g][:, e[g]] for g in range(8)])).reshape(128, -1)
def tile(rs):
    return np.stack(rs, axis=2).reshape(128, -1).astype(BF)
def pick(q, e):
    c = np.concatenate([q[0].reshape(128, -1, 4), np.zeros((128, 1, 4), np.uint8)], axis=1); s = np.concatenate([q[1], np.ones((16, 1), np.uint8)], axis=1)
    return (np.ascontiguousarray(c[:, e].reshape(128, -1)), np.ascontiguousarray(s[:, e]))
def join(*qs):
    return (np.concatenate([q[0] for q in qs], axis=1), np.concatenate([q[1] for q in qs], axis=1))
def put(q, e, v):
    c, s = q[0].reshape(128, -1, 4).copy(), q[1].copy(); c[:, e] = v[0].reshape(128, -1, 4); s[:, e] = v[1]
    return (c.reshape(128, -1), s)
def pk(c, s):
    return (np.ascontiguousarray(c), mx_ref.live(s))
def emit(q):
    return q[0], q[1]
def packed(v, rng):
    q = [mx_ref.quantize(np.ascontiguousarray(v[r])) for r in range(N)]
    return np.stack([a for a, b in q]), np.stack([mx_ref.plane(b, rng) for a, b in q])
def values_of_codes():
    e, c = np.zeros((128, 128, 4), np.float32), np.zeros((128, 2, 4), np.uint8)
    e[np.arange(128), np.arange(128), 0] = 1
    c[:127, :, 0] = np.arange(256).reshape(2, 128).T[:127]
    return mx_ref.matmul(mx_ref.quantize(e.reshape(128, 512).astype(BF)), (c.reshape(128, 8), np.full((16, 2), 127, np.uint8))).T.reshape(-1).astype(np.float64)
CODE_VALUE, SCALE_VALUE = values_of_codes(), 2.0 ** (np.arange(256) - 127.0)
def decode(q):
    return (CODE_VALUE[q[0]].reshape(16, 8, -1, 4) * SCALE_VALUE[q[1]][:, None, :, None] + 0.0).reshape(128, -1).astype(np.float32)
def f(rng, *shape):
    return mx_ref.flush((rng.standard_normal(shape, dtype=np.float32) * np.exp2(rng.integers(-2, 3, shape[:-1] + (1,)))).astype(BF))
def wide(rng, *shape, cols=0):
    v = rng.standard_normal(shape, dtype=np.float32) * np.exp2(rng.integers(-12, 13, shape)).astype(np.float32)
    if cols: v *= np.repeat(np.exp2(rng.integers(-cols, cols + 1, shape[:-2] + (1, shape[-1] // 4))) * (rng.random(shape[:-2] + (1, shape[-1] // 4)) > 0.0625), 4, axis=-1).astype(np.float32)
    return mx_ref.flush(v.astype(BF))
C = 320
TURN = [1, 2, 3]
def numbers_of(rng):
    return {"x": np.array(f(rng, N, 128, 4 * C)), "u": np.array(f(rng, N, 128, 512)), "v": np.array(f(rng, N, 128, 512))}
def rotors(rng):
    return np.argsort(rng.random((N, 8, C)), axis=2)
def stored(e):
    return np.stack([gtable(e[r]) for r in range(N)])
def layers(rng):
    return 2.0 * rng.random((N, 128, 4, 128, 4)) - 1.0
def kept(rng):
    w, i = layers(rng), np.arange(16)
    w[:, :, :, :16] = 0
    for b in range(4): w[:, i, b, i, b] = 1
    return w
def weights(rng, w):
    c, s = packed(np.ascontiguousarray(w).reshape(N, 128, 2048).astype(np.float32).astype(BF), rng)
    return {"wc": c, "ws": s}
def setup_inputs(rng):
    return {**numbers_of(rng), "p": stored(rotors(rng)), **weights(rng, layers(rng))}
def setup_inputs_ties(rng):
    d = numbers_of(rng)
    o = rng.permutation(N)
    k = rng.integers(-2, 3, (N, C))
    k[o[0]] = 1
    k[o[1]] = 0
    k[o[2]] = -1 - rng.integers(0, 2, C)
    x = d["x"].reshape(N, 128, C, 4)
    x[:, :16] = 0
    x[:, 0, :, 0] = k.astype(np.float32).astype(BF)
    u = d["u"].reshape(N, 128, 128, 4)
    u[:, :, 0] = 0
    u[:, :, 1::16] = 0
    for r in range(N):
        u[r, 0, 0, 0] = 1.0 if o[r] % 2 == 0 else -1.0
        u[r, 0, 1::16, 0] = rng.permutation([1, 1, 1, -1, -1, -1, 0, 0]).astype(np.float32).astype(BF)
    return {"x": x.reshape(N, 128, 4 * C), "u": u.reshape(N, 128, 512), "v": d["v"], "p": stored(rotors(rng)), **weights(rng, kept(rng))}
def setup_inputs_near(rng):
    d = numbers_of(rng)
    s = rng.integers(0, 16, (N, C))
    size = np.where(np.arange(N) // 2 % 2 == rng.integers(2), 2.0 ** 9, 2.0 ** -7)[:, None]
    x = d["x"].astype(np.float32).reshape(N, 128, C, 4)
    x[:, :16] = 0
    x[:, 0, :, 0] = rng.integers(-1, 2, (N, C)) * size
    x[:, 8] = ((s[:, :, None] >> np.arange(4)) & 1) * np.exp2(np.arange(4) - 23.0) * size[:, :, None]
    x[:, 11, :, 0] = 2.0 ** -10 * size
    u = d["u"].reshape(N, 128, 128, 4)
    u[:, :, 0] = 0
    u[:, :, 1::16] = 0
    w = kept(rng)
    odd = int(rng.integers(2))
    for r in range(N):
        k = 1.0 if r % 2 == odd else 2.0 ** -30
        if r % 2 != odd: w[r, :, :, :16] *= 0.0625
        u[r, 0, 0, 0] = k
        u[r, 8, 0] = k
        u[r, 11, 0, 0] = k
        h = rng.permutation(8)
        for g in range(8):
            if h[g] < 4: u[r, 8, 16 * g + 1] = k
            else: u[r, 0, 16 * g + 1, 0] = -k
    return {"x": x.reshape(N, 128, 4 * C).astype(BF), "u": u.reshape(N, 128, 512), "v": d["v"], "p": stored(rotors(rng)), **weights(rng, w)}
def setup_inputs_huge(rng):
    d = numbers_of(rng)
    o = rng.permutation(N)
    e = rotors(rng)
    e[o < N // 2, 1:] = np.arange(C)
    x = 2.0 ** 25 * (0.75 + 0.25 * rng.random((N, 128, C, 4)))
    x[o == 0] = 2.0 ** 25
    u = d["u"].reshape(N, 128, 128, 4)
    for r in range(N):
        k = rng.permutation(C)
        t = 1.0 - 0.125 * (k // 2 % 2)
        t = t * (k % 2 * 2.0 - 1.0) if o[r] < N // 2 else t * (o[r] % 2 * 2.0 - 1.0)
        x[r] *= t[None, :, None]
        u[r, :, 0] = ((rng.integers(2) * 2.0 - 1.0) * 2.0 ** 30 * (1.0 - 0.1 * rng.random((128, 4)))).astype(np.float32).astype(BF)
        u[r, :, 1::16] = ((rng.permutation(8) % 2 * 2.0 - 1.0)[None, :, None] * 2.0 ** 30 * (1.0 - 0.1 * rng.random((128, 8, 4)))).astype(np.float32).astype(BF)
    return {"x": x.astype(np.float32).reshape(N, 128, 4 * C).astype(BF), "u": u.reshape(N, 128, 512), "v": d["v"], "p": stored(e), **weights(rng, np.ones((N, 128, 4, 128, 4)))}
def setup_inputs_ends(rng):
    d = numbers_of(rng)
    o = rng.permutation(N)
    e = rotors(rng)
    i = np.arange(C)
    x = np.full((N, 128, C, 4), 2.0 ** 25)
    w = np.ones((N, 128, 4, 128, 4))
    u = d["u"].reshape(N, 128, 128, 4)
    for r in range(N):
        k = o[r] % 4
        if k == 0:
            e[r, 1:] = i
            x[r, :, rng.integers(C)] *= -1.0
        elif k == 2: e[r] = (i + C - 1) % C
        else:
            if k == 1: e[r] = i[::-1]
            x[r, 32:] *= rng.integers(0, 2, (96, C, 4)) * 2.0 - 1.0
            x[r, 64:] *= 2.0 ** -55
        x[r] *= rng.integers(2) * 2.0 - 1.0
        a = 2.0 ** -30 if o[r] == 1 else 2.0 ** 30
        u[r, :, 0] = a * (rng.integers(2) * 2.0 - 1.0)
        t = rng.permutation([1, 1, 1, 1, -1, -1, -1, 0]) * a
        u[r, :, 1::16] = t.astype(np.float32).astype(BF)[None, :, None]
        if o[r] == 3: w[r, 64:] = (rng.integers(0, 2, (64, 4, 128, 4)) * 2.0 - 1.0) * 2.0 ** -30
    d["v"] = (np.where(d["v"] < 0, -1.0, 1.0) * np.where(rng.permutation(N) % 2, 2.0 ** -30, 2.0 ** 30)[:, None, None]).astype(np.float32).astype(BF)
    return {"x": x.astype(np.float32).reshape(N, 128, 4 * C).astype(BF), "u": u.reshape(N, 128, 512), "v": d["v"], "p": stored(e), **weights(rng, w)}
def setup_inputs_spread(rng):
    d = setup_inputs(rng)
    d["x"] = wide(rng, N, 128, 4 * C, cols=6)
    return d
def check_inputs(d):
    b = []
    for k, top in (("x", 2.0 ** 25), ("u", 2.0 ** 30), ("v", 2.0 ** 30)):
        a = np.abs(d[k].astype(np.float32))
        if not (np.isfinite(a).all() and ((a == 0) | (a >= 2.0 ** -30) & (a <= top)).all()): b.append("a value of " + k)
    none, least, most = [emit(mx_ref.quantize(np.full((128, 16), k, np.float32).astype(BF)))[1][0, 0] for k in (0.0, 2.0 ** -30, 1.0)]
    for r in range(N):
        if (np.sort(gentries(d["p"][r]), axis=1) != np.arange(C)).any(): b.append("p: a group without a permutation")
        if ((d["wc"][r] & 0x7F) == 0x7F).any(): b.append("wc: a code that is no number")
        s = mx_ref.live(d["ws"][r])
        if ((s != none) & ((s < least) | (s > most))).any(): b.append("ws: a scale out of range")
        elif (np.abs(decode(pk(d["wc"][r], d["ws"][r]))) > 1).any(): b.append("a number of W beyond 1")
    return b
def reference(x, u, v, p, wc, ws):
    qu = [mx_ref.quantize(u[r]) for r in range(N)]
    lay = [pk(wc[r], ws[r]) for r in range(N)]
    rho = np.stack([gentries(p[r]) for r in range(N)])
    now = [x[r] for r in range(N)]
    a = np.zeros((N, 8), np.int64)
    op = np.zeros((N, 8, C), np.float32)
    for h in TURN:
        e = np.zeros((N, 8, C), np.int64)
        j = np.zeros((N, 1), np.int64) + np.arange(C)
        for g in range(8):
            j = (np.take_along_axis(rho[:, g], (j + a[:, g:g + 1]) % C, axis=1) - a[:, g:g + 1]) % C
            e[:, g] = j
        back = np.argsort(e, axis=2)
        for r in range(N):
            b = r ^ h
            part = gcols(now[r], e[r])
            q = mx_ref.quantize(part)
            z = mx_ref.quantize(tile([mx_ref.matmul(pick(lay[b], np.arange(128 * k, 128 * k + 128)), q) * np.float32(0.0078125) for k in range(4)]))
            s = mx_ref.matmul(qu[b], z) + np.float32(0.0)
            o = np.argsort(-s[0], kind="stable")
            m = np.zeros(C, np.int64)
            m[o[::2]] = o[1::2]
            m[o[1::2]] = o[::2]
            mixed = ((part.astype(np.float32) + decode(z)) * np.float32(0.5)).astype(BF)
            come = m[back[r]]
            now[r] = gcols(mixed, come)
            a[r] = (a[r] + np.sum(s[1::16] > 0, axis=1)) % C
            op[r] = (np.take_along_axis(e[r], come, axis=1) + a[r][:, None]) % C
    y = np.zeros((N, 128, C), np.float32)
    oc, osc = np.zeros((N, 128, 4 * C), np.uint8), np.zeros((N, 16, C), np.uint8)
    for r in range(N):
        q = mx_ref.quantize(now[r])
        y[r] = mx_ref.matmul(mx_ref.quantize(v[r]), q)
        oc[r], osc[r] = emit(q)
    return {"y": y, "op": op, "oc": oc, "osc": osc}

from concourse.mybir import dt, AluOpType as A, ActivationFunctionType as AF

C = 320
K = C // 16
HC = C // 2
TURN = [1, 2, 3]
NL = 192
UO, NO = 160, 180
HALF = (C - 1) / 2.0
WHOLE = 192.0
HOLD = 1024.0
WU = 512 + 144
RELAYED = 1

F32, BF, F16, I32, U16, Q4, U8 = "float32", "bfloat16", "float16", "int32", "uint16", "float8_e4m3fn_x4", "uint8"
SCRATCH = {
    "oq": ("sbuf", [128, WU], Q4), "osx": ("sbuf", [128, WU], U8),
    "uq": ("sbuf", [128, 128], Q4), "up": ("sbuf", [128, 128], U8),
    "rq": ("sbuf", [128, WU], Q4), "rp": ("sbuf", [128, WU], U8),
    "xs": ("sbuf", [128, 4 * C], BF), "us": ("sbuf", [128, 512], BF), "vs": ("sbuf", [128, 512], BF),
    "vq": ("sbuf", [128, 128], Q4), "vp": ("sbuf", [128, 128], U8),
    "pw": ("sbuf", [128, K], I32), "pr": ("sbuf", [128, 160], I32), "pu": ("sbuf", [128, K], U16),
    "pc": ("sbuf", [128, 8], I32), "ci": ("sbuf", [128, 8], I32), "cf": ("sbuf", [128, 16], F32),
    "iot": ("sbuf", [128, C], F32), "d0": ("sbuf", [128, 16], F32), "m1": ("sbuf", [128, 16], F32),
    "m2": ("sbuf", [128, 16], F32), "msk": ("sbuf", [128, C], F16),
    "n0": ("sbuf", [128, 160], F32), "s16": ("sbuf", [128, 160], F32), "iw": ("sbuf", [128, 160], F32),
    "iw2": ("sbuf", [128, 160], F32), "l0": ("sbuf", [128, 160], F32),
    "e0": ("sbuf", [128, 16], F32), "e1": ("sbuf", [128, 16], I32), "e2": ("sbuf", [128, 16], F32),
    "e3": ("sbuf", [128, 16], F32), "e4": ("sbuf", [128, 16], F32), "ex": ("sbuf", [128, 16], U16),
    "ul": ("sbuf", [128, 10], U16),
    "ls": ("sbuf", [128, NL], F16), "lx": ("sbuf", [128, NL], F16), "lt": ("sbuf", [128, NL], BF),
    "ly": ("sbuf", [128, NL], F16), "lu": ("sbuf", [128, NL], U16),
    "ea": ("sbuf", [128, K], F32), "eb": ("sbuf", [128, K], F32), "ec": ("sbuf", [128, K], F32), "eu": ("sbuf", [128, K], U16),
    "rho": ("sbuf", [128, C], F32), "w0": ("sbuf", [128, C], F32), "w1": ("sbuf", [128, C], F32), "wf": ("sbuf", [128, C], F16),
    "hold": ("sbuf", [128, C], F16), "uw": ("sbuf", [128, K], U16), "lw": ("sbuf", [128, 4 * K], U16), "rw": ("sbuf", [128, K], U16),
    "oo": ("sbuf", [128, C], F32), "ox": ("sbuf", [128, C], F32), "mm": ("sbuf", [128, C], F32),
    "sr": ("sbuf", [128, C], F32), "lr": ("sbuf", [128, C], F16), "ur": ("sbuf", [128, C], F32), "opr": ("sbuf", [128, C], F32),
    "ft": ("sbuf", [128, 4 * C], BF), "fq": ("sbuf", [128, C], Q4), "fp": ("sbuf", [128, C], U8),
    "ht": ("sbuf", [128, 4 * C], BF), "hq": ("sbuf", [128, C], Q4), "hp": ("sbuf", [128, C], U8),
    "zp": ("sbuf", [128, 4 * C], F32),
    "et": ("sbuf", [128, 2048], BF), "eq": ("sbuf", [128, 512], Q4), "ep": ("sbuf", [128, 512], U8),
    "ot": ("sbuf", [128, 1024], BF), "onq": ("sbuf", [128, 256], Q4), "onp": ("sbuf", [128, 256], U8),
    "fl": ("sbuf", [128, 4 * 136], BF), "flq": ("sbuf", [128, 136], Q4), "flp": ("sbuf", [128, 136], U8),
    "bt": ("sbuf", [128, 4 * C], BF), "bq": ("sbuf", [128, C], Q4), "bp": ("sbuf", [128, C], U8),
    "sg": ("sbuf", [128, 384], BF),
    "tri": ("sbuf", [128, 128], F32), "sc": ("sbuf", [128, 4], F32), "dl": ("sbuf", [128, 4], F32),
    "tiny": ("sbuf", [128, 4], F32), "thr": ("sbuf", [128, C], F32), "nd": ("sbuf", [128, 32], F32),
    "ys": ("sbuf", [128, C], F32),
    "pa": ("psum", [128, 2048], F32), "pb": ("psum", [128, 1536], F32), "pv": ("psum", [128, 512], F32),
}
for _t in range(3):
    SCRATCH["lq%d" % _t] = ("sbuf", [128, WU], Q4)
    SCRATCH["lp%d" % _t] = ("sbuf", [128, WU], U8)
SEMAPHORES = ["cv", "cs", "cp", "cg", "dws", "dwc", "dx", "du", "dv", "dp", "dpr", "aw0", "au0", "aw1", "aw2", "sent",
              "arel", "oy", "ooc", "oos", "oop"]


def relay_of(T, topo, rank):
    me, dst = T.cores[rank], T.cores[rank ^ TURN[RELAYED]]
    return [c for c in topo.cores_of(me) if topo.die(c) != topo.die(me) and T.rank_of(c) is None and topo.may_write(c, dst)][0]


def spare_mask(topo, core, near, far):
    m = 0
    for e in topo.engines(core, near):
        if e not in topo.engines(core, far):
            m += 1 << e
    return m


def relay_program(g, core, T, topo, rank):
    dst = T.cores[rank ^ TURN[RELAYED]]
    rid, pid, _ = topo.addr(dst)
    m = topo.mask(core, dst)
    g.wait_ge(T.sem.arel, 2 * bin(spare_mask(topo, T.cores[rank], core, dst)).count("1"))
    g.remote_dma(T["lq%d" % RELAYED][:].bitcast(dt.uint8), T.rq[:].bitcast(dt.uint8), T.sem["aw%d" % RELAYED], T.sem.sent, pid, rid, m)
    g.remote_dma(T["lp%d" % RELAYED][:], T.rp[:], T.sem["aw%d" % RELAYED], T.sem.sent, pid, rid, m)
    g.wait_ge(T.sem.sent, 2 * len(topo.engines(core, dst)))


def rank_program(g, core, T, topo):
    rank = T.rank_of(core)
    if rank is None:
        for r in range(len(T.cores)):
            if relay_of(T, topo, r) == core:
                relay_program(g, core, T, topo, r)
        return
    Q = {"V": g.vector, "S": g.scalar, "P": g.tensor, "G": g, "Y": g.sync}
    CS = {"V": "cv", "S": "cs", "P": "cp", "G": "cg"}
    cnt = {}
    known = {q: {} for q in Q}
    wr, rd, bank = {}, {}, {}
    seq = [0]

    def need(q, toks):
        for tok in sorted(toks, key=lambda t: -t[3]):
            if known[q].get(tok[0], 0) < tok[1]:
                Q[q].wait_ge(T.sem[tok[0]], tok[1])
                for s, v in tok[2].items():
                    if known[q].get(s, 0) < v:
                        known[q][s] = v

    def token(q, sem, n):
        cnt[sem] = cnt.get(sem, 0) + n
        seq[0] += 1
        clock = dict(known[q]) if q else {}
        clock[sem] = cnt[sem]
        return (sem, cnt[sem], clock, seq[0])

    def op(q, make, r=(), w=(), b=(), sem=None):
        toks = [wr[k] for k in list(r) + list(w) if k in wr]
        for k in w:
            toks += rd.get(k, [])
        for k in b:
            toks += [t for e, t in bank.get(k, {}).items() if e != q]
        need(q, toks)
        n = 16 if sem else 1
        tok = token(q, sem or CS[q], n)
        make().then_inc(T.sem[tok[0]], n)
        for k in r:
            rd.setdefault(k, []).append(tok)
        for k in w:
            wr[k] = tok
            rd[k] = []
        for k in b:
            bank.setdefault(k, {})[q] = tok
        return tok

    V, S, P = g.vector, g.scalar, g.tensor

    def ts(out, in0, s1, s2, o0, o1=None, **kw):
        if o1 is None:
            return op("V", lambda: V.tensor_scalar(out, in0, s1, None, o0), **kw)
        return op("V", lambda: V.tensor_scalar(out, in0, s1, s2, o0, o1), **kw)

    def tt(out, in0, in1, o, **kw):
        return op("V", lambda: V.tensor_tensor(out, in0, in1, o), **kw)

    def cp(out, in_, **kw):
        return op("V", lambda: V.tensor_copy(out, in_), **kw)

    def act(out, in_, f, kw2, **kw):
        return op("S", lambda: S.activation(out, in_, f, **kw2), **kw)

    def mset(ap, c, **kw):
        return op("V", lambda: V.memset(ap, c), **kw)

    def quant(q, s, t, **kw):
        return op("V", lambda: V.quantize_mx(q, s, t), **kw)

    def mx(out, lq, lp, rq, rp, start=True, stop=True, **kw):
        return op("P", lambda: P.matmul_mx(out, lq, lp, rq, rp, start, stop), **kw)

    def iota(out, pat, base, cm, flt=True, **kw):
        if flt:
            return op("G", lambda: g.iota(out, pat, base, cm, allow_small_or_imprecise_dtypes=True), **kw)
        return op("G", lambda: g.iota(out, pat, base, cm), **kw)

    def gather(q, out, win, off, scale=None, **kw):
        if q == "V":
            if scale is None:
                return cp(out, win.indirect(off), **kw)
            return ts(out, win.indirect(off), scale, None, A.mult, **kw)
        if scale is None:
            return act(out, win.indirect(off), AF.Copy, {}, **kw)
        return act(out, win.indirect(off), AF.Identity, {"scale": scale}, **kw)

    def scatter(win, off, row, **kw):
        return op("V", lambda: V.tensor_copy(win.indirect(off), row), **kw)

    def scan(row, **kw):
        r = list(kw.pop("r", [])) + ["msk"]
        return op("V", lambda: V.tensor_tensor_scan(T.hold[:], T.msk[:], row, 0.0, A.add, A.max), r=r, w=["hold"], **kw)

    def some(fills, n=1):
        for _ in range(n):
            if fills:
                fills.pop(0)()

    held = T.hold[:, 15:C:16]
    col = lambda buf, j: buf[:, j:j + 1]
    PF, G16, NG16, NG1, QF, GF, OFF, OFFH = [col(T.cf, j) for j in range(8)]
    NA = col(T.cf, 12)

    op("Y", lambda: g.sync.dma_start(T.osx[:, 0:512], T.ws[:]), w=["osw"], sem="dws")
    op("S", lambda: S.dma_start(T.pw[:], T.p[:]), w=["pw"], sem="dp")
    mset(T.pr[:], 0, w=["pr0"])
    for s in range(1, 8):
        q = "Y" if s < 4 else "S"
        tk = op(q, lambda: Q[q].dma_start(T.pr[16 * s:128, K * (s - 1):K * s], T.p[0:128 - 16 * s, :]), r=["pr0"], sem="dpr")
    wr["pr"] = tk
    op("Y", lambda: g.sync.dma_start(T.oq[:, 0:512].bitcast(dt.uint8), T.wc[:]), w=["oqw"], sem="dwc")
    op("S", lambda: S.dma_start(T.us[:], T.u[:]), w=["us"], sem="du")
    op("S", lambda: S.dma_start(T.xs[:], T.x[:]), w=["xs"], sem="dx")
    op("S", lambda: S.dma_start(T.vs[:], T.v[:]), w=["vs"], sem="dv")

    iota(col(T.pc, 0), [[0, 1]], 0, 1, flt=False, w=["pc"])
    iota(T.n0[:], [[0, 8], [16, K]], 0, 1, w=["n0"])
    iota(T.s16[:], [[16, 8], [0, K]], 16, -1, w=["s16"])
    iota(T.iot[:], [[1, C]], 0, 0, w=["iot"])
    iota(T.d0[:], [[1, 16]], 0, -1, w=["d0"])
    mset(T.ul[:], 0, w=["ul"])
    ts(col(T.ci, 0), col(T.pc, 0), 15, None, A.bitwise_and, r=["pc"], w=["ci0"])
    ts(col(T.ci, 1), col(T.pc, 0), 4, None, A.arith_shift_right, r=["pc"], w=["ci1"])
    cp(PF, col(T.pc, 0), r=["pc"], w=["PF"])
    cp(QF, col(T.ci, 0), r=["ci0"], w=["QF"])
    ts(G16, col(T.ci, 1), 16.0, None, A.mult, r=["ci1"], w=["G16"])
    ts(NG16, col(T.ci, 1), -16.0, None, A.mult, r=["ci1"], w=["NG16"])
    ts(NG1, col(T.ci, 1), -16.0, 1.0, A.mult, A.add, r=["ci1"], w=["NG1"])
    ts(col(T.ci, 2), QF, 8.0, QF, A.is_ge, A.add, r=["QF"], w=["ci2"])
    ts(T.iw[:], T.n0[:], G16, None, A.subtract, r=["n0", "G16"], w=["iw"])
    ts(col(T.ci, 3), col(T.ci, 2), 7, None, A.bitwise_and, r=["ci2"], w=["ci3"])
    ts(OFF, col(T.ci, 0), 15.0, HOLD, A.is_lt, A.mult, r=["ci0"], w=["OFF"])
    ts(T.l0[:], T.s16[:], 0.0, None, A.is_gt, r=["s16"], w=["l0"])
    ts(col(T.ul, 0), col(T.ci, 3), 16.0, 1.0, A.mult, A.add, r=["ci3"], w=["ul"])
    tt(T.iw2[:], T.iw[:], T.l0[:], A.mult, r=["iw", "l0"], w=["iw2"])
    mset(T.ot[:, 0:512], 1.0, w=["ot0"])
    cp(T.pu[:], T.pw[:], r=["pw"], w=["pu"])
    gather("S", T.rho[:], T.iot[:], T.pu[:], r=["iot", "pu"], w=["rho0", "rho1"])
    mset(T.ot[:, 512:1024], -1.0, w=["ot1"])
    tt(T.l0[:], T.pr[:], T.iw2[:], A.add, r=["pr", "iw2"], w=["l0"])
    cp(GF, col(T.ci, 1), r=["ci1"], w=["GF"])
    cp(T.lu[:, 0:160], T.l0[:], r=["l0"], w=["lu"])

    def chain(first, last, end, split):
        for s in range(first, last + 1):
            sn = "rho" if s == 1 else "w%d" % ((s - 1) % 2)
            dn = "wf" if s == end else "w%d" % (s % 2)
            o = K * (s - 1)
            sk = [sn + "0", sn + "1", "lu"]
            if split:
                gather("V", T[dn][:, 0:160], T[sn][:], T.lu[:, o:o + 10], r=sk, w=[dn + "0"])
                gather("S", T[dn][:, 160:C], T[sn][:], T.lu[:, o + 10:o + K], r=sk, w=[dn + "1"])
            else:
                gather("S", T[dn][:], T[sn][:], T.lu[:, o:o + K], r=sk, w=[dn + "0", dn + "1"])

    def widen(n):
        m = min(n, C - n)
        cp(T.msk[:, n:n + m], T.msk[:, 0:m], r=["msk"], w=["msk"])

    chain(1, 6, 7, False)
    ts(T.m1[:], T.d0[:], NG16, -4.0 * HOLD, A.is_le, A.mult, r=["d0", "NG16"], w=["m1"])
    ts(T.m2[:], T.d0[:], NG1, HOLD, A.is_equal, A.mult, r=["d0", "NG1"], w=["m2"])
    mset(T.fl[:], 0.0, w=["fl0", "fl1", "fl2"])
    tt(T.msk[:, 0:16], T.m1[:], T.m2[:], A.add, r=["m1", "m2"], w=["msk"])
    quant(T.onq[:], T.onp[:], T.ot[:], r=["ot0", "ot1"], w=["onq"])
    mset(T.bt[:, 3:4 * C:4], 0.0, w=["btz"])
    mset(T.bt[0:64, 2:4 * C:4], 0.0, w=["bty"])
    ts(T.ls[:, NO:NL], T.iot[:, 0:NL - NO], 0.0, -HALF, A.mult, A.add, r=["iot"], w=["lsn"])
    ts(T.tri[:], T.iot[:, 0:128], PF, None, A.is_gt, r=["iot", "PF"], w=["tri"])
    quant(T.uq[:], T.up[:], T.us[:], r=["us"], w=["uq"])
    widen(16)
    cp(T.osx[:, 512:WU], T.up[:].indirect(T.ul[:, 0:9]), r=["uq", "ul"], w=["osu"])
    cp(T.oq[:, 512:WU].bitcast(dt.uint32), T.uq[:].bitcast(dt.uint32).indirect(T.ul[:, 0:9]), r=["uq", "ul"], w=["oqu"])

    def put(dst, m, out, in_, sem, deps):
        rid, pid, _ = topo.addr(dst)
        need("G", [wr[k] for k in deps])
        g.remote_dma(out, in_, T.sem[sem], T.sem.sent, pid, rid, m)
        cnt["sent"] = cnt.get("sent", 0) + bin(m).count("1")

    def send(dst, m, q, p, a, b, sem, dq, dp):
        put(dst, m, p[:, a:b], T.osx[:, a:b], sem, dp)
        put(dst, m, q[:, a:b].bitcast(dt.uint8), T.oq[:, a:b].bitcast(dt.uint8), sem, dq)

    peer = [T.cores[rank ^ h] for h in TURN]
    send(peer[0], topo.mask(core, peer[0]), T.lq0, T.lp0, 0, 512, "aw0", ["oqw"], ["osw"])
    send(peer[0], topo.mask(core, peer[0]), T.lq0, T.lp0, 512, WU, "au0", ["oqu"], ["osu"])
    rel = relay_of(T, topo, rank)
    send(rel, spare_mask(topo, core, rel, peer[RELAYED]), T.rq, T.rp, 0, WU, "arel", [], [])
    for b in range(4):
        op("G", lambda: g.affine_select(T.et[:, 512 * b:512 * (b + 1)], T.ot[:, 0:512], [[8, 128], [1, 4]], A.is_equal, 0.0, -b, -8),
           r=["ot0"], w=["et%d" % b])
    g.wait_ge(T.sem.sent, cnt["sent"])
    send(peer[2], topo.mask(core, peer[2]), T.lq2, T.lp2, 0, WU, "aw2", [], [])
    wr["W0"] = token(None, "aw0", 2 * len(topo.engines(peer[0], core)))
    wr["U0"] = token(None, "au0", 2 * len(topo.engines(peer[0], core)))
    wr["W1"] = wr["U1"] = token(None, "aw1", 2 * len(topo.engines(relay_of(T, topo, rank ^ TURN[RELAYED]), core)))
    wr["W2"] = wr["U2"] = token(None, "aw2", 2 * len(topo.engines(peer[2], core)))

    widen(32)
    ts(OFFH, OFF, HALF, None, A.add, r=["OFF"], w=["OFFH"])
    ts(T.e0[:, 0:10], T.iw[:, 0:10], -(K - 1) / 2.0, 1.0 / K, A.add, A.mult, r=["iw"], w=["e0"])
    widen(64)
    ts(col(T.e0, 12), GF, 0.0, 8.0, A.is_equal, A.mult, r=["GF"], w=["e012"])
    cp(T.e1[:, 0:10], T.e0[:, 0:10], r=["e0"], w=["e1"])
    widen(128)
    ts(col(T.e0, 13), col(T.e0, 12), 15.0, None, A.add, r=["e012"], w=["e013"])
    ts(T.e2[:, 0:10], T.e1[:, 0:10], -1.0, GF, A.mult, A.add, r=["e1", "GF"], w=["e2"])
    widen(256)
    for t in range(4):
        ts(col(T.cf, 8 + t), OFF, -4.0, float(t), A.mult, A.add, r=["OFF"], w=["O4%d" % t])
    ts(T.e3[:, 0:10], T.e2[:, 0:10], 1.0, None, A.is_ge, r=["e2"], w=["e3"])
    ts(T.e4[:, 0:10], T.e2[:, 0:10], 7.0, None, A.add, r=["e2"], w=["e4"])
    ts(T.e0[:, 0:10], T.e2[:, 0:10], -1.0, 24.0, A.is_le, A.mult, r=["e2"], w=["e0"])
    ts(col(T.e0, 14), QF, 4.0, col(T.e0, 13), A.is_ge, A.mult, r=["QF", "e013"], w=["e014"])
    tt(T.e2[:, 0:10], T.e3[:, 0:10], T.e4[:, 0:10], A.mult, r=["e3", "e4"], w=["e2"])
    cp(col(T.ex, 10), GF, r=["GF"], w=["ex10"])
    ts(col(T.ex, 11), col(T.e0, 14), GF, None, A.add, r=["e014", "GF"], w=["ex11"])
    tt(T.e3[:, 0:10], T.e2[:, 0:10], T.e0[:, 0:10], A.add, r=["e2", "e0"], w=["e3"])
    ts(T.ls[:, 0:160], T.l0[:], -HALF, None, A.add, r=["l0"], w=["lss"])
    cp(T.ex[:, 0:10], T.e3[:, 0:10], r=["e3"], w=["ex"])
    EXK = ["ex", "ex10", "ex11"]

    chain(7, 7, 7, True)
    scan(T.wf[:], r=["wf0", "wf1"])
    mset(T.tiny[:], 2.0 ** -120, w=["tiny"])
    for t in (0, 2, 1, 3):
        ts(T.lw[:, K * t:K * (t + 1)], held, 4.0, col(T.cf, 8 + t), A.mult, A.add, r=["hold", "O4%d" % t], w=["lw%d" % t])

    def half(buf, h, n=1):
        return buf[:, n * HC * h:n * HC * (h + 1)]

    def psum(i, n):
        return T.pa[:, 512 * i:512 * i + n] if i < 4 else T.pb[:, 512 * (i - 4):512 * (i - 4) + n] if i < 7 else T.pv[:, 0:n]

    def quant_e(b):
        quant(T.eq[:, 128 * b:128 * (b + 1)], T.ep[:, 128 * b:128 * (b + 1)], T.et[:, 512 * b:512 * (b + 1)], r=["et%d" % b], w=["eq%d" % b])

    def make_tile(first, fill):
        for b in range(4):
            for h, q in enumerate("VS"):
                out = T.ft[:, 4 * HC * h + b:4 * HC * (h + 1):4]
                if first:
                    gather(q, out, T.xs[:], T.lw[:, K * b + 10 * h:K * b + 10 * h + 10], r=["xs", "lw%d" % b], w=["ft%d%d" % (b, h)])
                else:
                    gather(q, out, T.zp[:, C * b:C * (b + 1)], T.lw[:, 10 * h:10 * h + 10], 0.5, r=["zp%d0" % b, "zp%d1" % b, "lw0"], w=["ft%d%d" % (b, h)])
        fill()
        for h in range(2):
            quant(half(T.fq, h), half(T.fp, h), half(T.ft, h, 4), r=["ft%d%d" % (b, h) for b in range(4)], w=["fq%d" % h])

    HQ = ["hq0", "hq1"]
    for t in range(3):
        last = t == 2
        lq, lp, uk = T["lq%d" % t], T["lp%d" % t], "U%d" % t
        if t == 0:
            make_tile(True, lambda: ts(T.ls[:, UO:NO], held, OFFH, None, A.subtract, r=["hold", "OFFH"], w=["lsu"]))
        else:
            make_tile(False, lambda: ts(T.ls[:, UO:NO], T.uw[:], HALF, None, A.subtract, r=["uw"], w=["lsu"]))
        for h in range(2):
            for k in range(4):
                mx(psum(4 * h + k, HC), lq[:, 128 * k:128 * (k + 1)], lp[:, 128 * k:128 * (k + 1)], half(T.fq, h), half(T.fp, h),
                   r=["fq%d" % h, "W%d" % t], b=[4 * h + k])
        fills = []
        if t == 0:
            quant_e(0)
            fills = [lambda: None, lambda: quant_e(1)]
        if t == 1:
            quant(T.vq[:], T.vp[:], T.vs[:], r=["vs"], w=["vq"])
        if last:
            cp(NA, col(T.ls, NO), r=["lsn"], w=["NA"])
            ts(T.ea[:], T.uw[:], NA, None, A.add, r=["uw", "NA"], w=["ea"])
            fills = [lambda: ts(T.eb[:], T.ea[:], HALF + 1.0, -float(C), A.is_ge, A.mult, r=["ea"], w=["eb"]),
                     lambda: tt(T.ec[:], T.ea[:], T.eb[:], A.add, r=["ea", "eb"], w=["ec"])]
        for h in range(2):
            for k in range(4):
                out, src_ = T.ht[:, 4 * HC * h + k:4 * HC * (h + 1):4], psum(4 * h + k, HC)
                if k % 2 == 0 or (h, k) == (1, 1):
                    act(out, src_, AF.Identity, {"scale": 0.0078125}, w=["ht%d%d" % (k, h)], b=[4 * h + k])
                else:
                    ts(out, src_, 0.0078125, None, A.mult, w=["ht%d%d" % (k, h)], b=[4 * h + k])
            if t > 0:
                some(fills)
            quant(half(T.hq, h), half(T.hp, h), half(T.ht, h, 4), r=["ht%d%d" % (k, h) for k in range(4)], w=["hq%d" % h])
            if t == 0:
                some(fills)
        if last:
            ts(T.eu[:], T.ec[:], HALF, None, A.add, r=["ec"], w=["eu"])
        for c, a in enumerate((0, 128, 192)):
            mx(T.pb[:, 512 * c:512 * c + 128], T.hq[:, a:a + 128], T.hp[:, a:a + 128], lq[:, 512:640], lp[:, 512:640],
               r=(HQ if c else HQ[:1]) + [uk], b=[4 + c])
        mx(T.pv[:, 0:C], lq[:, 528:WU], lp[:, 528:WU], T.hq[:], T.hp[:], r=HQ + [uk], b=[7])

        def flags():
            for c in range(3):
                p0 = 64 if c == 2 else 0
                ts(T.fl[p0:128, 32 + c:96:4], T.pb[p0:128, 512 * c:512 * c + 16], 0.0, None, A.is_gt, w=["fl%d" % c], b=[4 + c])

        def counts():
            quant(T.flq[:], T.flp[:], T.fl[:], r=["fl0", "fl1", "fl2"], w=["flq"])
            mx(T.pb[:, 0:128], T.onq[:, 0:128], T.onp[:, 0:128], T.flq[:, 8:136], T.flp[:, 8:136], True, False, r=["flq", "onq"], b=[4])
            mx(T.pb[:, 0:128], T.onq[:, 128:256], T.onp[:, 128:256], T.flq[:, 0:128], T.flp[:, 0:128], False, True, r=["flq", "onq"], b=[4])

        def second_row(n):
            mx(psum(3, n), lq[:, 528:WU], lp[:, 528:WU], T.hq[:, 0:n], T.hp[:, 0:n], r=HQ + [uk], b=[3])

        def unpack(bs):
            for b in bs:
                mx(psum(b, C), T.eq[:, 128 * b:128 * (b + 1)], T.ep[:, 128 * b:128 * (b + 1)], T.hq[:], T.hp[:],
                   r=HQ + ["eq%d" % b], b=[b])

        def thr(c, p0, a, n, o):
            act(T.thr[p0:128, a:a + n], T.tri[p0:128, o:o + n], AF.Identity,
                {"scale": T.dl[p0:128, c:c + 1], "bias": T.sc[p0:128, c:c + 1]}, r=["tri", "dl", "sc"], w=["thr%d" % c])

        def above(c, p0, n, o, key):
            act(T.sg[p0:128, o:o + n], T.pa[p0:128, 1536:1536 + n], AF.Sign, {"scale": -1.0, "bias": T.sc[p0:128, c:c + 1]},
                r=["sc"], w=["sg%d" % c], b=[3])
            return lambda: act(T.bt[p0:128, c:4 * n:4], T.sg[p0:128, o:o + n], AF.Relu, {}, r=["sg%d" % c], w=[key])

        def cmp_s(c, a, e, key):
            return lambda: ts(T.bt[:, 4 * a + c:4 * e:4], T.pv[:, a:e], T.sc[:, c:c + 1], None, A.is_le, r=["sc"], w=[key], b=[7])

        def cmp_t(c, p0, a, e, key):
            return lambda: tt(T.bt[p0:128, 4 * a + c:4 * e:4], T.pv[p0:128, a:e], T.thr[p0:128, a:e], A.is_lt, r=["thr%d" % c], w=[key], b=[7])

        def zadd(b, h):
            return lambda: tt(T.zp[:, C * b + HC * h:C * b + HC * (h + 1)], T.ft[:, 4 * HC * h + b:4 * HC * (h + 1):4],
                              T.pa[:, 512 * b + HC * h:512 * b + HC * (h + 1)], A.add, r=["ft%d%d" % (b, h)], w=["zp%d%d" % (b, h)], b=[b])

        def swap_on_pool(o):
            op("G", lambda: g.affine_select(T.ox[:, o:C:2], T.oo[:, 1 - o:C:2], [[0, C // 2]], A.is_ge, 0.0, 0, 0), r=["oo"], w=["ox%d" % o])

        a, e = (UO, NL) if last else (0, NL)
        lk = ["lsu", "lsn"] if last else ["lss", "lsu", "lsn"]
        steps = [
            lambda: tt(T.lx[:, a:e], T.nd[:].indirect(T.ex[:, a // 16:e // 16]), T.ls[:, a:e], A.add, r=["nd"] + EXK + lk, w=["lx"]),
            lambda: ts(T.lt[:, a:e], T.lx[:, a:e], 1.0 / C, WHOLE, A.mult, A.add, r=["lx"], w=["lt"]),
            lambda: ts(T.ly[:, a:e], T.lt[:, a:e], -WHOLE, -float(C), A.add, A.mult, r=["lt"], w=["ly"]),
            lambda: tt(T.ls[:, a:e], T.lx[:, a:e], T.ly[:, a:e], A.add, r=["lx", "ly"], w=lk),
            lambda: ts(T.lu[:, a:e], T.ls[:, a:e], HALF, None, A.add, r=lk, w=["lu"]),
        ]
        nd = lambda: act(T.nd[:], T.pb[:, 0:32], AF.Copy, {}, w=["nd"], b=[4])
        scores = lambda: cp(T.sc[:, 0:3], T.pb[:, 16:1536:512], w=["sc"], b=[4, 5, 6])
        delta = lambda: act(T.dl[:, 0:3], T.sc[:, 0:3], AF.Abs, {"scale": 0.625 * 2.0 ** -23, "bias": col(T.tiny, 0)}, r=["sc", "tiny"], w=["dl"])
        cmps = [cmp_s(0, 128, C, "bt1"), cmp_s(1, 256, C, "bt5"), cmp_t(0, 0, 0, 128, "bt3"), cmp_t(2, 64, 256, C, "bt6"), cmp_t(1, 0, 128, 256, "bt4")]
        zs = [zadd(b, h) for b in range(4) for h in range(2)]

        def ranks():
            quant(T.bq[:], T.bp[:], T.bt[:], r=["bt%d" % i for i in range(7)] + ["btz", "bty"], w=["bq"])
            mx(psum(7, C), T.onq[:, 0:128], T.onp[:, 0:128], T.bq[:], T.bp[:], r=["bq", "onq"], b=[7])

        if not last:
            second_row(256)
            flags()
            scores()
            counts()
            unpack([0, 1])
            delta()
            thr(0, 0, 0, 128, 0)
            nd()
            thr(2, 64, 256, 64, 64)
            thr(1, 0, 128, 128, 0)
            r2 = above(2, 64, 256, 128, "bt0")
            r1 = above(1, 0, 128, 0, "bt2")
            r2()
            r1()
            some(cmps, 3)
            if t > 0:
                unpack([2, 3])
            for i in range(4):
                some(steps)
                some(cmps if cmps else zs if i == 3 else [])
            some(steps)
            chain(1, 8, 8, False)
            ranks()
            if t == 0:
                quant_e(2)
                quant_e(3)
                unpack([2, 3])
            else:
                some(zs, 2)
            scan(psum(7, C), b=[7])
            some(zs)
            ts(T.rw[:], held, OFF, None, A.subtract, r=["hold", "OFF"], w=["rw"])
            some(zs)
            scatter(T.oo[:], T.rw[:], T.iot[:], r=["rw", "iot"], w=["oo"])
            swap_on_pool(0)
            some(zs)
            cp(T.ox[:, 1:C:2], T.oo[:, 0:C:2], r=["oo"], w=["ox1"])
            some(zs, 2 if t == 0 else 1)
            gather("V", T.mm[:], T.ox[:], T.rw[:], r=["ox0", "ox1", "rw"], w=["mm"])
            some(zs)
            scatter(T.sr[:], T.lu[:, UO:NO], T.mm[:], r=["lu", "mm"], w=["sr"])
            scan(T.wf[:], r=["wf0", "wf1"])
            some(zs)
            ts(T.uw[:], held, OFF, None, A.subtract, r=["hold", "OFF"], w=["uw"])
            gather("V", T.lr[:, 0:160], T.sr[:], T.uw[:, 0:10], r=["sr", "uw"], w=["lr0"])
            gather("S", T.lr[:, 160:C], T.sr[:], T.uw[:, 10:K], r=["sr", "uw"], w=["lr1"])
            scan(T.lr[:], r=["lr0", "lr1"])
        else:
            second_row(128)
            scores()
            unpack([0, 1, 2])
            delta()
            thr(0, 0, 0, 128, 0)
            thr(2, 64, 256, 64, 64)
            thr(1, 0, 128, 128, 0)
            above(1, 0, 128, 0, "bt2")()
            unpack([3])
            ts(T.bt[64:128, 2:4 * 256:4], T.pv[64:128, 0:256], T.sc[64:128, 2:3], None, A.is_lt, r=["sc"], w=["bt0"], b=[7])
            some(cmps, 5)
            ranks()
            some(zs, 2)
            scan(psum(7, C), b=[7])
            flags()
            ts(T.rw[:], held, OFF, None, A.subtract, r=["hold", "OFF"], w=["rw"])
            counts()
            nd()
            scatter(T.oo[:], T.rw[:], T.iot[:], r=["rw", "iot"], w=["oo"])
            act(T.ox[:, 0:C:2], T.oo[:, 1:C:2], AF.Copy, {}, r=["oo"], w=["ox0"])
            act(T.ox[:, 1:C:2], T.oo[:, 0:C:2], AF.Copy, {}, r=["oo"], w=["ox1"])
            gather("S", T.mm[:], T.ox[:], T.rw[:], r=["ox0", "ox1", "rw"], w=["mm"])
            for _ in range(3):
                some(steps)
                some(zs, 2)
            some(steps)
            scatter(T.sr[:], T.eu[:], T.mm[:], r=["eu", "mm"], w=["sr"])
            some(steps)
            scan(T.sr[:], r=["sr"])
            gather("S", T.ur[:], T.iot[:], T.lu[:, UO:NO], r=["iot", "lu"], w=["ur"])
        ts(T.lw[:, 0:K], held, OFF, None, A.subtract, r=["hold", "OFF"], w=["lw0"])

    make_tile(False, lambda: None)
    for h in range(2):
        mx(psum(6 + h, HC), T.vq[:], T.vp[:], half(T.fq, h), half(T.fp, h), r=["fq%d" % h, "vq"], b=[6 + h])
        op("Y", lambda: g.sync.dma_start(half(T.oc, h, 4), half(T.fq, h).bitcast(dt.uint8)), r=["fq%d" % h], sem="ooc")
    gather("S", T.opr[:], T.ur[:], T.lw[:, 0:K], r=["ur", "lw0"], w=["opr"])
    for h in range(2):
        cp(half(T.ys, h), psum(6 + h, HC), w=["ys%d" % h], b=[6 + h])
        op("Y", lambda: g.sync.dma_start(half(T.y, h), half(T.ys, h)), r=["ys%d" % h], sem="oy")
    for k in range(4):
        op("S", lambda: S.dma_start(T.osc[4 * k:4 * k + 4, :], T.fp[32 * k:32 * k + 4, :]), r=["fq0", "fq1"], sem="oos")
    op("S", lambda: S.dma_start(T.op[:], T.opr[0:128:16, :]), r=["opr"], sem="oop")
    for s, v in cnt.items():
        g.wait_ge(T.sem[s], v)
